import numpy as np
import ml_dtypes


def mxq(x, axis, fmt="e4m3"):
    dtype, down = {"e4m3": (ml_dtypes.float8_e4m3fn, 7), "e5m2": (ml_dtypes.float8_e5m2, 14)}[fmt]
    v = np.moveaxis(np.asarray(x, np.float32).astype(ml_dtypes.bfloat16).astype(np.float64), axis, -1)
    blocks = v.reshape(v.shape[:-1] + (-1, 32))
    amax = np.abs(blocks).max(-1, keepdims=True)
    byte = np.maximum(np.where(amax > 0, np.frexp(amax)[1] - 1 + 127, 0) - down, 1)
    scale = np.exp2(byte - 127.0)
    codes = (blocks / scale).astype(np.float32).astype(dtype).astype(np.float64)
    return np.moveaxis((codes * scale).reshape(v.shape), -1, axis)


WIDE = False


def mx_kscale(k):
    if not WIDE:
        return np.ones(k)
    levels = np.array([10, -10, 5, -5, 0])
    if k % 512:
        return np.exp2(np.random.permutation(np.resize(levels, k // 32))).repeat(32)
    a = np.empty((k // 512, 16))
    for p in range(k // 512):
        a[p, :8] = np.random.permutation(np.resize(levels, 8))
        for g in range(8):
            far = levels[np.abs(levels - a[p, g]) >= 10]
            a[p, g + 8] = far[np.random.randint(len(far))]
    return np.exp2(a.ravel()).repeat(32)


def f64(x):
    return np.asarray(x).astype(np.float64)


def striped8(idx):
    return np.asarray(idx).reshape(8, -1, 16).transpose(0, 2, 1).reshape(128, -1).astype(np.uint16)


def unstriped8(offs):
    return offs.reshape(8, 16, -1).transpose(0, 2, 1).reshape(8, -1).astype(np.int64)


def pick8(x, idx, run):
    r = np.arange(len(x))
    return x[r[:, None], idx[r % (8 * run) // run]]


E2M1 = np.array([0.0, 0.5, 1.0, 1.5, 2.0, 3.0, 4.0, 6.0, -0.0, -0.5, -1.0, -1.5, -2.0, -3.0, -4.0, -6.0])


def pack_weight(w, fmt):
    k, n = w.shape
    w = f64(np.asarray(w, np.float32).astype(ml_dtypes.bfloat16)).reshape(k // 32, 32, n)
    amax = np.abs(w).max(1)
    if fmt == "e4m3":
        byte = np.frexp(amax)[1] - 1 + 127 - 7
    else:
        mant, ex = np.frexp(amax / 6.0)
        byte = np.where(mant > 0.5, ex, ex - 1) + 127
    byte = np.clip(np.where(amax > 0, byte, 1), 1, 254)
    scaled = (w * np.exp2(127.0 - byte)[:, None, :]).reshape(k, n).astype(np.float32)
    by_word = np.ascontiguousarray(scaled.reshape(k // 512, 128, 4, n).transpose(0, 1, 3, 2))
    if fmt == "e4m3":
        words = by_word.astype(ml_dtypes.float8_e4m3fn).view(np.uint8)
    else:
        c = by_word.astype(ml_dtypes.float4_e2m1fn).view(np.uint8) & 0xF
        words = (c[..., 0::2] | (c[..., 1::2] << 4)).reshape(k // 512, 128, 2 * n)
    return np.ascontiguousarray(words), np.ascontiguousarray(byte.astype(np.uint8).reshape(k // 512, 16, n))


def unpack_weight(words, scales, fmt):
    g, _, n = scales.shape
    words = np.ascontiguousarray(words).reshape(g, 128, n, -1)
    if fmt == "e4m3":
        vals = words.view(ml_dtypes.float8_e4m3fn).astype(np.float64)
    else:
        nib = np.empty((g, 128, n, 4), np.uint8)
        nib[..., 0::2] = words & 0xF
        nib[..., 1::2] = words >> 4
        vals = E2M1[nib]
    vals = vals * np.repeat(np.exp2(scales.astype(np.float64) - 127.0), 8, axis=1)[..., None]
    return vals.transpose(0, 1, 3, 2).reshape(g * 512, n)


D, K, T, U, X, I, Q = 512, 512, 1024, 1024, 1024, 512, 128


def setup_inputs():
    n = np.random.standard_normal
    idx = np.stack([np.random.permutation(T)[:I] for _ in range(8)])
    idx2 = np.stack([np.random.permutation(U)[:I] for _ in range(8)])
    idx3 = np.stack([np.random.permutation(X)[:I] for _ in range(8)])
    idx4 = np.stack([np.random.permutation(U)[:I] for _ in range(8)])
    idx5 = np.stack([np.random.permutation(U)[:I] for _ in range(8)])
    idx6 = np.stack([np.random.permutation(X)[:I] for _ in range(8)])
    fd = mx_kscale(D)
    fk = mx_kscale(K)
    wqp = pack_weight(n((D, K)) * 1.0 / np.sqrt(D) * fd[:, None] * fk, "e4m3")
    keysp = pack_weight(n((K, T)) * 1.0 / np.sqrt(K) / fk[:, None], "e2m1")
    notesp = pack_weight(n((K, U)) * 1.0 / np.sqrt(K) / fk[:, None], "e4m3")
    usersp = pack_weight(n((D, X)) * 1.0 / np.sqrt(D) * fd[:, None], "e2m1")
    return {
        "states": (n((D, Q)) * 0.95 / fd[:, None]).astype(np.float32),
        "wq_words": wqp[0],
        "wq_scales": wqp[1],
        "keys_words": keysp[0],
        "keys_scales": keysp[1],
        "notes_words": notesp[0],
        "notes_scales": notesp[1],
        "users_words": usersp[0],
        "users_scales": usersp[1],
        "offs": striped8(idx),
        "offs2": striped8(idx2),
        "offs3": striped8(idx3),
        "offs4": striped8(idx4),
        "offs5": striped8(idx5),
        "offs6": striped8(idx6),
    }


def reference(states, wq_words, wq_scales, keys_words, keys_scales, notes_words, notes_scales, users_words, users_scales, offs, offs2, offs3, offs4, offs5, offs6):
    idx = unstriped8(offs)
    idx2 = unstriped8(offs2)
    idx3 = unstriped8(offs3)
    idx4 = unstriped8(offs4)
    idx5 = unstriped8(offs5)
    idx6 = unstriped8(offs6)
    wqu = unpack_weight(wq_words, wq_scales, "e4m3")
    keysu = unpack_weight(keys_words, keys_scales, "e2m1")
    notesu = unpack_weight(notes_words, notes_scales, "e4m3")
    usersu = unpack_weight(users_words, users_scales, "e2m1")
    statesq = mxq(f64(states), 0, "e4m3")
    qv = wqu.T @ statesq
    qvq = mxq(qv, 0, "e4m3")
    a = qvq.T @ keysu
    b = qvq.T @ notesu
    c0 = statesq.T @ usersu
    w = pick8(a, idx, 16) - pick8(b, idx2, 16)
    v = pick8(c0, idx3, 16) - pick8(a, idx, 16)
    f1 = np.zeros((Q, X))
    f1[np.arange(Q)[:, None], idx3[np.arange(Q) % 128 // 16]] = w
    f2 = np.zeros((Q, U))
    f2[np.arange(Q)[:, None], idx4[np.arange(Q) % 128 // 16]] = v
    bb = b + f2
    cc = c0 + f1
    y = np.maximum(pick8(bb, idx5, 16), pick8(cc, idx6, 16))
    return y

@@ -1,0 +1,169 @@
+from contextlib import ExitStack
+
+import concourse.mybir as mybir
+
+D, K, T, Q, SLOTS = 512, 512, 1024, 128, 512
+P = 128
+PACK = 4
+BANK = 512
+HALF = SLOTS // 2
+FLOPS = 2 * D * K * Q + 3 * 2 * K * Q * T
+
+F32 = mybir.dt.float32
+BF16 = mybir.dt.bfloat16
+I32 = mybir.dt.int32
+U32 = mybir.dt.uint32
+U16 = mybir.dt.uint16
+U8 = mybir.dt.uint8
+FP8X4 = mybir.dt.float8_e4m3fn_x4
+FP4X4 = mybir.dt.float4_e2m1fn_x4
+ALU = mybir.AluOpType
+COPY = mybir.ActivationFunctionType.Copy
+
+
+def load_scale_rows(queue, plane, scales):
+    for quadrant in range(4):
+        queue.dma_start(
+            out=plane[32 * quadrant : 32 * quadrant + 4, :].bitcast(I32),
+            in_=scales[0, 4 * quadrant : 4 * quadrant + 4, :].bitcast(I32),
+        )
+
+
+def tile_attend_twoerrands_madethree_kernel(
+    tc, states, wq_words, wq_scales, keys_words, keys_scales, notes_words, notes_scales,
+    users_words, users_scales, offs, offs2, offs3, offs4, offs5, offs6, out,
+):
+    nc = tc.nc
+    with ExitStack() as ctx:
+        sb = ctx.enter_context(tc.tile_pool(name="sb", bufs=1))
+        ps = ctx.enter_context(tc.psum_pool(name="ps", bufs=1))
+
+        states_raw = sb.tile([P, PACK, Q], F32, name="states_raw", align_bytes=64)
+        wq_raw = sb.tile([P, K], U32, name="wq_raw", align_bytes=64)
+        wq_plane_raw = sb.tile([P, K], U8, name="wq_plane_raw", align_bytes=64)
+        keys_codes = sb.tile([P, 2 * T], U8, name="keys_codes", align_bytes=64)
+        users_codes = sb.tile([P, 2 * T], U8, name="users_codes", align_bytes=64)
+        notes_codes = sb.tile([P, T], U32, name="notes_codes", align_bytes=64)
+        keys_plane = sb.tile([P, T], U8, name="keys_plane", align_bytes=64)
+        users_plane = sb.tile([P, T], U8, name="users_plane", align_bytes=64)
+        notes_plane = sb.tile([P, T], U8, name="notes_plane", align_bytes=64)
+        lists = [sb.tile([P, SLOTS // 16], U16, name="list%d" % n) for n in range(6)]
+        idx, idx2, idx3, idx4, idx5, idx6 = lists
+        f1 = sb.tile([P, T], F32, name="f1")
+        f2 = sb.tile([P, T], F32, name="f2")
+
+        for plane in (wq_plane_raw, users_plane, keys_plane, notes_plane):
+            nc.gpsimd.memset(plane[:].bitcast(I32), 0)
+        nc.vector.memset(f2[:], 0.0)
+        nc.vector.memset(f1[:], 0.0)
+
+        nc.sync.dma_start(out=states_raw[:], in_=states.rearrange("(p t) q -> p t q", t=PACK))
+        load_scale_rows(nc.scalar, wq_plane_raw, wq_scales)
+        nc.sync.dma_start(out=wq_raw[:].bitcast(I32), in_=wq_words[0].rearrange("p n t -> p (n t)").bitcast(I32))
+        nc.sync.dma_start(out=users_codes[:].bitcast(I32), in_=users_words[0].bitcast(I32))
+        load_scale_rows(nc.sync, users_plane, users_scales)
+        nc.sync.dma_start(out=keys_codes[:].bitcast(I32), in_=keys_words[0].bitcast(I32))
+        load_scale_rows(nc.sync, keys_plane, keys_scales)
+        nc.sync.dma_start(idx3[:], offs3)
+        nc.sync.dma_start(idx[:], offs)
+        nc.sync.dma_start(out=notes_codes[:].bitcast(I32), in_=notes_words[0].rearrange("p n t -> p (n t)").bitcast(I32))
+        nc.sync.dma_start(idx4[:], offs4)
+        load_scale_rows(nc.sync, notes_plane, notes_scales)
+        nc.sync.dma_start(idx2[:], offs2)
+        nc.sync.dma_start(idx5[:], offs5)
+        nc.sync.dma_start(idx6[:], offs6)
+
+        wq_codes = sb.tile([P, K], U32, name="wq_codes", align_bytes=64)
+        wq_plane = sb.tile([P, K], U8, name="wq_plane", align_bytes=64)
+        nc.vector.tensor_copy(
+            out=wq_plane[:].rearrange("p (t c i) -> p c t i", t=PACK, i=16),
+            in_=wq_plane_raw[:].rearrange("p (c i t) -> p c t i", t=PACK, i=16),
+        )
+        nc.scalar.copy(
+            out=wq_codes[:].rearrange("p (t c i) -> p c t i", t=PACK, i=4),
+            in_=wq_raw[:].rearrange("p (c i t) -> p c t i", t=PACK, i=4),
+        )
+
+        states_bf = sb.tile([P, Q, PACK], BF16, name="states_bf", align_bytes=64)
+        nc.vector.tensor_copy(
+            out=states_bf[:].rearrange("p (c i) t -> p c t i", i=4),
+            in_=states_raw[:].rearrange("p t (c i) -> p c t i", i=4),
+        )
+        states_codes = sb.tile([P, Q], U32, name="states_codes", align_bytes=64)
+        states_plane = sb.tile([P, Q], U8, name="states_plane", align_bytes=64)
+        nc.vector.quantize_mx(
+            out=states_codes[:].bitcast(FP8X4), scales=states_plane[:],
+            in_=states_bf[:].rearrange("p q t -> p (q t)"),
+        )
+
+        qv_ps = ps.tile([P, PACK, Q], F32, name="qv_ps")
+        for t in range(PACK):
+            cols = slice(t * P, (t + 1) * P)
+            nc.tensor.matmul_mx(
+                out=qv_ps[:, t, :], lhsT=wq_codes[:, cols].bitcast(FP8X4), lhsT_scale=wq_plane[:, cols],
+                rhs=states_codes[:].bitcast(FP8X4), rhs_scale=states_plane[:], start=True, stop=True,
+            )
+        qv_bf = sb.tile([P, Q, PACK], BF16, name="qv_bf", align_bytes=64)
+        nc.vector.tensor_copy(out=qv_bf[:], in_=qv_ps[:].rearrange("p t q -> p q t"))
+        qv_codes = sb.tile([P, Q], U32, name="qv_codes", align_bytes=64)
+        qv_plane = sb.tile([P, Q], U8, name="qv_plane", align_bytes=64)
+        nc.vector.quantize_mx(
+            out=qv_codes[:].bitcast(FP8X4), scales=qv_plane[:],
+            in_=qv_bf[:].rearrange("p q t -> p (q t)"),
+        )
+
+        def scores(name, pieces, codes, plane, table, table_plane, is_fp4):
+            whole = sb.tile([P, T], F32, name=name)
+            start = 0
+            for n, (width, engine) in enumerate(pieces):
+                bank = ps.tile([P, width], F32, name="%s_ps%d" % (name, n))
+                if is_fp4:
+                    moving = table[:, 2 * start : 2 * (start + width)].bitcast(FP4X4)
+                else:
+                    moving = table[:, start : start + width].bitcast(FP8X4)
+                nc.tensor.matmul_mx(
+                    out=bank[:], lhsT=codes[:].bitcast(FP8X4), lhsT_scale=plane[:],
+                    rhs=moving, rhs_scale=table_plane[:, start : start + width], start=True, stop=True,
+                )
+                if engine == "vector":
+                    nc.vector.tensor_copy(out=whole[:, start : start + width], in_=bank[:])
+                else:
+                    nc.scalar.copy(out=whole[:, start : start + width], in_=bank[:])
+                start += width
+            return whole
+
+        lo, hi = slice(0, HALF), slice(HALF, SLOTS)
+        lo16, hi16 = slice(0, HALF // 16), slice(HALF // 16, SLOTS // 16)
+
+        c0 = scores("c0", [(BANK, "scalar"), (BANK, "vector")], states_codes, states_plane, users_codes, users_plane, True)
+        c0_picked = sb.tile([P, SLOTS], F32, name="c0_picked")
+        nc.vector.tensor_copy(c0_picked[:, lo], c0[:].indirect(idx3[:, lo16]))
+        nc.scalar.activation(c0_picked[:, hi], c0[:].indirect(idx3[:, hi16]), COPY)
+
+        a = scores("a", [(BANK, "scalar"), (BANK // 2, "vector"), (BANK // 2, "vector")], qv_codes, qv_plane, keys_codes, keys_plane, True)
+        a_neg = sb.tile([P, SLOTS], F32, name="a_neg")
+        nc.vector.tensor_scalar(a_neg[:, lo], a[:].indirect(idx[:, lo16]), -1.0, 0.0, ALU.mult, ALU.add)
+        nc.scalar.activation(a_neg[:, hi], a[:].indirect(idx[:, hi16]), COPY, scale=-1.0)
+        nc.vector.tensor_tensor(f2[:].indirect(idx4[:]), c0_picked[:], a_neg[:], ALU.add)
+
+        b = scores("b", [(BANK, "scalar"), (BANK, "scalar")], qv_codes, qv_plane, notes_codes, notes_plane, False)
+        b_neg = sb.tile([P, SLOTS], F32, name="b_neg")
+        nc.scalar.activation(b_neg[:], b[:].indirect(idx2[:]), COPY, scale=-1.0)
+        a_picked = sb.tile([P, SLOTS], F32, name="a_picked")
+        nc.scalar.activation(a_picked[:], a_neg[:], COPY, scale=-1.0)
+        nc.vector.tensor_tensor(f1[:].indirect(idx3[:]), a_picked[:], b_neg[:], ALU.add)
+
+        bb = sb.tile([P, T], F32, name="bb")
+        nc.vector.tensor_tensor(bb[:], b[:], f2[:], ALU.add)
+        cc = sb.tile([P, T], F32, name="cc")
+        nc.vector.tensor_tensor(cc[:], c0[:], f1[:], ALU.add)
+
+        bb_picked = sb.tile([P, SLOTS], F32, name="bb_picked")
+        nc.scalar.activation(bb_picked[:], bb[:].indirect(idx5[:]), COPY)
+        cc_picked = sb.tile([P, SLOTS], F32, name="cc_picked")
+        nc.vector.tensor_copy(cc_picked[:, lo], cc[:].indirect(idx6[:, lo16]))
+        nc.scalar.activation(cc_picked[:, hi], cc[:].indirect(idx6[:, hi16]), COPY)
+        result = sb.tile([P, SLOTS], F32, name="result")
+        for part in (lo, hi):
+            nc.vector.tensor_tensor(result[:, part], cc_picked[:, part], bb_picked[:, part], ALU.max)
+            nc.sync.dma_start(out=out[:, part], in_=result[:, part])

@@ -1,6 +1,7 @@
 from contextlib import ExitStack
 
 import concourse.mybir as mybir
+from concourse.masks import make_identity
 
 D, K, T, Q, SLOTS = 512, 512, 1024, 128, 512
 P = 128
@@ -21,8 +22,8 @@ ALU = mybir.AluOpType
 COPY = mybir.ActivationFunctionType.Copy
 
 
-def load_scale_rows(queue, plane, scales):
-    for quadrant in range(4):
+def load_scale_rows(queues, plane, scales):
+    for quadrant, queue in enumerate(queues):
         queue.dma_start(
             out=plane[32 * quadrant : 32 * quadrant + 4, :].bitcast(I32),
             in_=scales[0, 4 * quadrant : 4 * quadrant + 4, :].bitcast(I32),
@@ -36,11 +37,12 @@ def tile_attend_twoerrands_madethree_kernel(
     nc = tc.nc
     with ExitStack() as ctx:
         sb = ctx.enter_context(tc.tile_pool(name="sb", bufs=1))
+        reused = ctx.enter_context(tc.tile_pool(name="reused", bufs=1))
         ps = ctx.enter_context(tc.psum_pool(name="ps", bufs=1))
 
         states_raw = sb.tile([P, PACK, Q], F32, name="states_raw", align_bytes=64)
         wq_raw = sb.tile([P, K], U32, name="wq_raw", align_bytes=64)
-        wq_plane_raw = sb.tile([P, K], U8, name="wq_plane_raw", align_bytes=64)
+        wq_plane_raw = reused.tile([P, K], U8, name="wq_plane_raw", align_bytes=64, offset=1024)
         keys_codes = sb.tile([P, 2 * T], U8, name="keys_codes", align_bytes=64)
         users_codes = sb.tile([P, 2 * T], U8, name="users_codes", align_bytes=64)
         notes_codes = sb.tile([P, T], U32, name="notes_codes", align_bytes=64)
@@ -49,26 +51,24 @@ def tile_attend_twoerrands_madethree_kernel(
         notes_plane = sb.tile([P, T], U8, name="notes_plane", align_bytes=64)
         lists = [sb.tile([P, SLOTS // 16], U16, name="list%d" % n) for n in range(6)]
         idx, idx2, idx3, idx4, idx5, idx6 = lists
-        f1 = sb.tile([P, T], F32, name="f1")
-        f2 = sb.tile([P, T], F32, name="f2")
 
-        for plane in (wq_plane_raw, users_plane, keys_plane, notes_plane):
+        for plane in (wq_plane_raw, keys_plane):
             nc.gpsimd.memset(plane[:].bitcast(I32), 0)
-        nc.vector.memset(f2[:], 0.0)
-        nc.vector.memset(f1[:], 0.0)
+        for plane in (users_plane, notes_plane):
+            nc.vector.memset(plane[:].bitcast(I32), 0)
 
-        nc.sync.dma_start(out=states_raw[:], in_=states.rearrange("(p t) q -> p t q", t=PACK))
-        load_scale_rows(nc.scalar, wq_plane_raw, wq_scales)
         nc.sync.dma_start(out=wq_raw[:].bitcast(I32), in_=wq_words[0].rearrange("p n t -> p (n t)").bitcast(I32))
-        nc.sync.dma_start(out=users_codes[:].bitcast(I32), in_=users_words[0].bitcast(I32))
-        load_scale_rows(nc.sync, users_plane, users_scales)
-        nc.sync.dma_start(out=keys_codes[:].bitcast(I32), in_=keys_words[0].bitcast(I32))
-        load_scale_rows(nc.sync, keys_plane, keys_scales)
+        load_scale_rows([nc.sync] * 4, wq_plane_raw, wq_scales)
+        nc.sync.dma_start(out=states_raw[:], in_=states.rearrange("(p t) q -> p t q", t=PACK))
         nc.sync.dma_start(idx3[:], offs3)
+        nc.sync.dma_start(out=users_codes[:].bitcast(I32), in_=users_words[0].bitcast(I32))
+        load_scale_rows([nc.sync] * 4, users_plane, users_scales)
+        nc.sync.dma_start(out=keys_codes[:].bitcast(I32), in_=keys_words[0].bitcast(I32))
+        load_scale_rows([nc.sync] * 2 + [nc.gpsimd] * 2, keys_plane, keys_scales)
         nc.sync.dma_start(idx[:], offs)
         nc.sync.dma_start(out=notes_codes[:].bitcast(I32), in_=notes_words[0].rearrange("p n t -> p (n t)").bitcast(I32))
+        load_scale_rows([nc.sync] * 4, notes_plane, notes_scales)
         nc.sync.dma_start(idx4[:], offs4)
-        load_scale_rows(nc.sync, notes_plane, notes_scales)
         nc.sync.dma_start(idx2[:], offs2)
         nc.sync.dma_start(idx5[:], offs5)
         nc.sync.dma_start(idx6[:], offs6)
@@ -84,7 +84,7 @@ def tile_attend_twoerrands_madethree_kernel(
             in_=wq_raw[:].rearrange("p (c i t) -> p c t i", t=PACK, i=4),
         )
 
-        states_bf = sb.tile([P, Q, PACK], BF16, name="states_bf", align_bytes=64)
+        states_bf = reused.tile([P, Q, PACK], BF16, name="states_bf", align_bytes=64, offset=0)
         nc.vector.tensor_copy(
             out=states_bf[:].rearrange("p (c i) t -> p c t i", i=4),
             in_=states_raw[:].rearrange("p t (c i) -> p c t i", i=4),
@@ -96,7 +96,12 @@ def tile_attend_twoerrands_madethree_kernel(
             in_=states_bf[:].rearrange("p q t -> p (q t)"),
         )
 
-        qv_ps = ps.tile([P, PACK, Q], F32, name="qv_ps")
+        f2 = reused.tile([P, T], F32, name="f2", align_bytes=64, offset=0)
+        nc.vector.memset(f2[:], 0.0)
+        identity = sb.tile([P, P], F32, name="identity")
+        make_identity(nc, identity[:])
+
+        qv_ps = ps.tile([P, PACK, Q], F32, name="qv_ps", tag="bank0")
         for t in range(PACK):
             cols = slice(t * P, (t + 1) * P)
             nc.tensor.matmul_mx(
@@ -104,19 +109,18 @@ def tile_attend_twoerrands_madethree_kernel(
                 rhs=states_codes[:].bitcast(FP8X4), rhs_scale=states_plane[:], start=True, stop=True,
             )
         qv_bf = sb.tile([P, Q, PACK], BF16, name="qv_bf", align_bytes=64)
-        nc.vector.tensor_copy(out=qv_bf[:], in_=qv_ps[:].rearrange("p t q -> p q t"))
-        qv_codes = sb.tile([P, Q], U32, name="qv_codes", align_bytes=64)
+        nc.scalar.copy(out=qv_bf[:], in_=qv_ps[:].rearrange("p t q -> p q t"))
+        qv_codes = sb.tile([P, Q], U32, name="qv_codes", tag="f1", align_bytes=64)
         qv_plane = sb.tile([P, Q], U8, name="qv_plane", align_bytes=64)
         nc.vector.quantize_mx(
             out=qv_codes[:].bitcast(FP8X4), scales=qv_plane[:],
             in_=qv_bf[:].rearrange("p q t -> p (q t)"),
         )
 
-        def scores(name, pieces, codes, plane, table, table_plane, is_fp4):
-            whole = sb.tile([P, T], F32, name=name)
+        def scores(whole, pieces, codes, plane, table, table_plane, is_fp4):
             start = 0
-            for n, (width, engine) in enumerate(pieces):
-                bank = ps.tile([P, width], F32, name="%s_ps%d" % (name, n))
+            for width, engine, tag in pieces:
+                bank = ps.tile([P, width], F32, name="scores_bank", tag=tag)
                 if is_fp4:
                     moving = table[:, 2 * start : 2 * (start + width)].bitcast(FP4X4)
                 else:
@@ -130,40 +134,63 @@ def tile_attend_twoerrands_madethree_kernel(
                 else:
                     nc.scalar.copy(out=whole[:, start : start + width], in_=bank[:])
                 start += width
-            return whole
 
         lo, hi = slice(0, HALF), slice(HALF, SLOTS)
         lo16, hi16 = slice(0, HALF // 16), slice(HALF // 16, SLOTS // 16)
 
-        c0 = scores("c0", [(BANK, "scalar"), (BANK, "vector")], states_codes, states_plane, users_codes, users_plane, True)
-        c0_picked = sb.tile([P, SLOTS], F32, name="c0_picked")
-        nc.vector.tensor_copy(c0_picked[:, lo], c0[:].indirect(idx3[:, lo16]))
-        nc.scalar.activation(c0_picked[:, hi], c0[:].indirect(idx3[:, hi16]), COPY)
+        c0 = sb.tile([P, T], F32, name="c0")
+        scores(c0, [(BANK, "scalar", "bank1"), (BANK // 2, "vector", "bank2"), (BANK // 2, "scalar", "bank3")], states_codes, states_plane, users_codes, users_plane, True)
+        c0_lo = sb.tile([P, HALF], F32, name="c0_lo")
+        nc.scalar.activation(c0_lo[:], c0[:].indirect(idx3[:, lo16]), COPY)
 
-        a = scores("a", [(BANK, "scalar"), (BANK // 2, "vector"), (BANK // 2, "vector")], qv_codes, qv_plane, keys_codes, keys_plane, True)
+        a = reused.tile([P, T], F32, name="a", align_bytes=64, offset=4096)
+        scores(a, [(BANK, "vector", "bank4"), (BANK // 2, "vector", "bank5"), (BANK // 2, "scalar", "bank6")], qv_codes, qv_plane, keys_codes, keys_plane, True)
         a_neg = sb.tile([P, SLOTS], F32, name="a_neg")
-        nc.vector.tensor_scalar(a_neg[:, lo], a[:].indirect(idx[:, lo16]), -1.0, 0.0, ALU.mult, ALU.add)
-        nc.scalar.activation(a_neg[:, hi], a[:].indirect(idx[:, hi16]), COPY, scale=-1.0)
-        nc.vector.tensor_tensor(f2[:].indirect(idx4[:]), c0_picked[:], a_neg[:], ALU.add)
+        nc.scalar.activation(a_neg[:, lo], a[:].indirect(idx[:, lo16]), COPY, scale=-1.0)
+        nc.vector.tensor_scalar(a_neg[:, hi], a[:].indirect(idx[:, hi16]), -1.0, 0.0, ALU.mult, ALU.add)
+        nc.vector.tensor_tensor(f2[:].indirect(idx4[:, lo16]), c0_lo[:], a_neg[:, lo], ALU.add)
+        c0_hi = reused.tile([P, HALF], F32, name="c0_hi", align_bytes=64, offset=4096)
+        nc.scalar.activation(c0_hi[:], c0[:].indirect(idx3[:, hi16]), COPY)
+        nc.vector.tensor_tensor(f2[:].indirect(idx4[:, hi16]), c0_hi[:], a_neg[:, hi], ALU.add)
 
-        b = scores("b", [(BANK, "scalar"), (BANK, "scalar")], qv_codes, qv_plane, notes_codes, notes_plane, False)
+        b = reused.tile([P, T], F32, name="b", align_bytes=64, offset=4096 + 1024)
+        scores(b, [(BANK, "scalar", "bank7"), (BANK, "scalar", "bank0")], qv_codes, qv_plane, notes_codes, notes_plane, False)
+        f1 = sb.tile([P, T], F32, name="f1", tag="f1", align_bytes=64)
+        nc.gpsimd.memset(f1[:], 0.0)
         b_neg = sb.tile([P, SLOTS], F32, name="b_neg")
         nc.scalar.activation(b_neg[:], b[:].indirect(idx2[:]), COPY, scale=-1.0)
         a_picked = sb.tile([P, SLOTS], F32, name="a_picked")
         nc.scalar.activation(a_picked[:], a_neg[:], COPY, scale=-1.0)
         nc.vector.tensor_tensor(f1[:].indirect(idx3[:]), a_picked[:], b_neg[:], ALU.add)
 
-        bb = sb.tile([P, T], F32, name="bb")
-        nc.vector.tensor_tensor(bb[:], b[:], f2[:], ALU.add)
+        bb = sb.tile([P, T], F32, name="bb", tag="bb")
+        bb_turned = sb.tile([P, T], F32, name="bb_turned")
+        PIECE = 256
+        turned = [ps.tile([P, PIECE], F32, name="turned%d" % n, tag=tag) for n, tag in enumerate(("bank3", "bank4", "bank5", "bank6"))]
+        for term in (b, f2):
+            for h in range(4):
+                for j in range(2):
+                    nc.tensor.matmul(
+                        turned[h][:, j * P : (j + 1) * P], term[:, h * PIECE + j * P : h * PIECE + (j + 1) * P], identity[:],
+                        start=(term is b and j == 0), stop=(term is f2 and j == 1), is_transpose=True,
+                    )
+        for h in range(4):
+            nc.scalar.copy(out=bb_turned[:, h * PIECE : (h + 1) * PIECE], in_=turned[h][:])
+        for h, tag in enumerate(("bank7", "bank0", "bank3", "bank4")):
+            back = ps.tile([P, PIECE], F32, name="back%d" % h, tag=tag)
+            for j in range(2):
+                nc.tensor.transpose(back[:, j * P : (j + 1) * P], bb_turned[:, h * PIECE + j * P : h * PIECE + (j + 1) * P], identity[:])
+            nc.scalar.copy(out=bb[:, h * PIECE : (h + 1) * PIECE], in_=back[:])
         cc = sb.tile([P, T], F32, name="cc")
         nc.vector.tensor_tensor(cc[:], c0[:], f1[:], ALU.add)
 
         bb_picked = sb.tile([P, SLOTS], F32, name="bb_picked")
         nc.scalar.activation(bb_picked[:], bb[:].indirect(idx5[:]), COPY)
-        cc_picked = sb.tile([P, SLOTS], F32, name="cc_picked")
-        nc.vector.tensor_copy(cc_picked[:, lo], cc[:].indirect(idx6[:, lo16]))
-        nc.scalar.activation(cc_picked[:, hi], cc[:].indirect(idx6[:, hi16]), COPY)
+        cc_lo = sb.tile([P, HALF], F32, name="cc_lo")
+        cc_hi = sb.tile([P, HALF], F32, name="cc_hi", tag="bb")
+        nc.vector.tensor_copy(cc_lo[:], cc[:].indirect(idx6[:, lo16]))
+        nc.scalar.activation(cc_hi[:], cc[:].indirect(idx6[:, hi16]), COPY)
         result = sb.tile([P, SLOTS], F32, name="result")
-        for part in (lo, hi):
-            nc.vector.tensor_tensor(result[:, part], cc_picked[:, part], bb_picked[:, part], ALU.max)
+        for part, cc_picked in ((lo, cc_lo), (hi, cc_hi)):
+            nc.vector.tensor_tensor(result[:, part], cc_picked[:], bb_picked[:, part], ALU.max)
             nc.sync.dma_start(out=out[:, part], in_=result[:, part])

@@ -42,7 +42,7 @@ def tile_attend_twoerrands_madethree_kernel(
 
         states_raw = sb.tile([P, PACK, Q], F32, name="states_raw", align_bytes=64)
         wq_raw = sb.tile([P, K], U32, name="wq_raw", align_bytes=64)
-        wq_plane_raw = reused.tile([P, K], U8, name="wq_plane_raw", align_bytes=64, offset=1024)
+        wq_plane_raw = sb.tile([P, K], U8, name="wq_plane_raw", align_bytes=64)
         keys_codes = sb.tile([P, 2 * T], U8, name="keys_codes", align_bytes=64)
         users_codes = sb.tile([P, 2 * T], U8, name="users_codes", align_bytes=64)
         notes_codes = sb.tile([P, T], U32, name="notes_codes", align_bytes=64)
@@ -56,6 +56,10 @@ def tile_attend_twoerrands_madethree_kernel(
             nc.gpsimd.memset(plane[:].bitcast(I32), 0)
         for plane in (users_plane, notes_plane):
             nc.vector.memset(plane[:].bitcast(I32), 0)
+        f1 = sb.tile([P, T], F32, name="f1")
+        f2 = sb.tile([P, T], F32, name="f2")
+        nc.vector.memset(f2[:], 0.0)
+        nc.vector.memset(f1[:], 0.0)
 
         nc.sync.dma_start(out=wq_raw[:].bitcast(I32), in_=wq_words[0].rearrange("p n t -> p (n t)").bitcast(I32))
         load_scale_rows([nc.sync] * 4, wq_plane_raw, wq_scales)
@@ -84,7 +88,7 @@ def tile_attend_twoerrands_madethree_kernel(
             in_=wq_raw[:].rearrange("p (c i t) -> p c t i", t=PACK, i=4),
         )
 
-        states_bf = reused.tile([P, Q, PACK], BF16, name="states_bf", align_bytes=64, offset=0)
+        states_bf = sb.tile([P, Q, PACK], BF16, name="states_bf", align_bytes=64)
         nc.vector.tensor_copy(
             out=states_bf[:].rearrange("p (c i) t -> p c t i", i=4),
             in_=states_raw[:].rearrange("p t (c i) -> p c t i", i=4),
@@ -96,8 +100,6 @@ def tile_attend_twoerrands_madethree_kernel(
             in_=states_bf[:].rearrange("p q t -> p (q t)"),
         )
 
-        f2 = reused.tile([P, T], F32, name="f2", align_bytes=64, offset=0)
-        nc.vector.memset(f2[:], 0.0)
         identity = sb.tile([P, P], F32, name="identity")
         make_identity(nc, identity[:])
 
@@ -110,7 +112,7 @@ def tile_attend_twoerrands_madethree_kernel(
             )
         qv_bf = sb.tile([P, Q, PACK], BF16, name="qv_bf", align_bytes=64)
         nc.scalar.copy(out=qv_bf[:], in_=qv_ps[:].rearrange("p t q -> p q t"))
-        qv_codes = sb.tile([P, Q], U32, name="qv_codes", tag="f1", align_bytes=64)
+        qv_codes = sb.tile([P, Q], U32, name="qv_codes", align_bytes=64)
         qv_plane = sb.tile([P, Q], U8, name="qv_plane", align_bytes=64)
         nc.vector.quantize_mx(
             out=qv_codes[:].bitcast(FP8X4), scales=qv_plane[:],
@@ -143,20 +145,18 @@ def tile_attend_twoerrands_madethree_kernel(
         c0_lo = sb.tile([P, HALF], F32, name="c0_lo")
         nc.scalar.activation(c0_lo[:], c0[:].indirect(idx3[:, lo16]), COPY)
 
-        a = reused.tile([P, T], F32, name="a", align_bytes=64, offset=4096)
+        a = reused.tile([P, T], F32, name="a", align_bytes=64, offset=0)
         scores(a, [(BANK, "vector", "bank4"), (BANK // 2, "vector", "bank5"), (BANK // 2, "scalar", "bank6")], qv_codes, qv_plane, keys_codes, keys_plane, True)
         a_neg = sb.tile([P, SLOTS], F32, name="a_neg")
         nc.scalar.activation(a_neg[:, lo], a[:].indirect(idx[:, lo16]), COPY, scale=-1.0)
         nc.vector.tensor_scalar(a_neg[:, hi], a[:].indirect(idx[:, hi16]), -1.0, 0.0, ALU.mult, ALU.add)
         nc.vector.tensor_tensor(f2[:].indirect(idx4[:, lo16]), c0_lo[:], a_neg[:, lo], ALU.add)
-        c0_hi = reused.tile([P, HALF], F32, name="c0_hi", align_bytes=64, offset=4096)
+        c0_hi = reused.tile([P, HALF], F32, name="c0_hi", align_bytes=64, offset=0)
         nc.scalar.activation(c0_hi[:], c0[:].indirect(idx3[:, hi16]), COPY)
         nc.vector.tensor_tensor(f2[:].indirect(idx4[:, hi16]), c0_hi[:], a_neg[:, hi], ALU.add)
 
-        b = reused.tile([P, T], F32, name="b", align_bytes=64, offset=4096 + 1024)
+        b = reused.tile([P, T], F32, name="b", align_bytes=64, offset=1024)
         scores(b, [(BANK, "scalar", "bank7"), (BANK, "scalar", "bank0")], qv_codes, qv_plane, notes_codes, notes_plane, False)
-        f1 = sb.tile([P, T], F32, name="f1", tag="f1", align_bytes=64)
-        nc.gpsimd.memset(f1[:], 0.0)
         b_neg = sb.tile([P, SLOTS], F32, name="b_neg")
         nc.scalar.activation(b_neg[:], b[:].indirect(idx2[:]), COPY, scale=-1.0)
         a_picked = sb.tile([P, SLOTS], F32, name="a_picked")

@@ -88,7 +88,7 @@ def tile_attend_twoerrands_madethree_kernel(
             in_=wq_raw[:].rearrange("p (c i t) -> p c t i", t=PACK, i=4),
         )
 
-        states_bf = sb.tile([P, Q, PACK], BF16, name="states_bf", align_bytes=64)
+        states_bf = sb.tile([P, Q, PACK], BF16, name="states_bf", tag="states_bf", align_bytes=64)
         nc.vector.tensor_copy(
             out=states_bf[:].rearrange("p (c i) t -> p c t i", i=4),
             in_=states_raw[:].rearrange("p t (c i) -> p c t i", i=4),
@@ -100,7 +100,7 @@ def tile_attend_twoerrands_madethree_kernel(
             in_=states_bf[:].rearrange("p q t -> p (q t)"),
         )
 
-        identity = sb.tile([P, P], F32, name="identity")
+        identity = sb.tile([P, P], F32, name="identity", tag="states_bf", align_bytes=64)
         make_identity(nc, identity[:])
 
         qv_ps = ps.tile([P, PACK, Q], F32, name="qv_ps", tag="bank0")
@@ -121,6 +121,7 @@ def tile_attend_twoerrands_madethree_kernel(
 
         def scores(whole, pieces, codes, plane, table, table_plane, is_fp4):
             start = 0
+            banks = []
             for width, engine, tag in pieces:
                 bank = ps.tile([P, width], F32, name="scores_bank", tag=tag)
                 if is_fp4:
@@ -136,12 +137,14 @@ def tile_attend_twoerrands_madethree_kernel(
                 else:
                     nc.scalar.copy(out=whole[:, start : start + width], in_=bank[:])
                 start += width
+                banks.append(bank)
+            return banks
 
         lo, hi = slice(0, HALF), slice(HALF, SLOTS)
         lo16, hi16 = slice(0, HALF // 16), slice(HALF // 16, SLOTS // 16)
 
         c0 = sb.tile([P, T], F32, name="c0")
-        scores(c0, [(BANK, "scalar", "bank1"), (BANK // 2, "vector", "bank2"), (BANK // 2, "scalar", "bank3")], states_codes, states_plane, users_codes, users_plane, True)
+        c0_banks = scores(c0, [(BANK, "scalar", "bank1"), (BANK // 2, "vector", "bank2"), (BANK // 2, "scalar", "bank3")], states_codes, states_plane, users_codes, users_plane, True)
         c0_lo = sb.tile([P, HALF], F32, name="c0_lo")
         nc.scalar.activation(c0_lo[:], c0[:].indirect(idx3[:, lo16]), COPY)
 
@@ -156,7 +159,7 @@ def tile_attend_twoerrands_madethree_kernel(
         nc.vector.tensor_tensor(f2[:].indirect(idx4[:, hi16]), c0_hi[:], a_neg[:, hi], ALU.add)
 
         b = reused.tile([P, T], F32, name="b", align_bytes=64, offset=1024)
-        scores(b, [(BANK, "scalar", "bank7"), (BANK, "scalar", "bank0")], qv_codes, qv_plane, notes_codes, notes_plane, False)
+        scores(b, [(BANK, "scalar", "bank7"), (BANK // 2, "scalar", "bank0"), (BANK // 2, "vector", "bank3")], qv_codes, qv_plane, notes_codes, notes_plane, False)
         b_neg = sb.tile([P, SLOTS], F32, name="b_neg")
         nc.scalar.activation(b_neg[:], b[:].indirect(idx2[:]), COPY, scale=-1.0)
         a_picked = sb.tile([P, SLOTS], F32, name="a_picked")
@@ -182,7 +185,9 @@ def tile_attend_twoerrands_madethree_kernel(
                 nc.tensor.transpose(back[:, j * P : (j + 1) * P], bb_turned[:, h * PIECE + j * P : h * PIECE + (j + 1) * P], identity[:])
             nc.scalar.copy(out=bb[:, h * PIECE : (h + 1) * PIECE], in_=back[:])
         cc = sb.tile([P, T], F32, name="cc")
-        nc.vector.tensor_tensor(cc[:], c0[:], f1[:], ALU.add)
+        nc.vector.tensor_tensor(cc[:, 0:512], c0_banks[0][:], f1[:, 0:512], ALU.add)
+        nc.vector.tensor_tensor(cc[:, 512:768], c0_banks[1][:], f1[:, 512:768], ALU.add)
+        nc.gpsimd.tensor_tensor(cc[:, 768:1024], c0[:, 768:1024], f1[:, 768:1024], ALU.add)
 
         bb_picked = sb.tile([P, SLOTS], F32, name="bb_picked")
         nc.scalar.activation(bb_picked[:], bb[:].indirect(idx5[:]), COPY)

@@ -64,11 +64,11 @@ def tile_attend_twoerrands_madethree_kernel(
         nc.sync.dma_start(out=wq_raw[:].bitcast(I32), in_=wq_words[0].rearrange("p n t -> p (n t)").bitcast(I32))
         load_scale_rows([nc.sync] * 4, wq_plane_raw, wq_scales)
         nc.sync.dma_start(out=states_raw[:], in_=states.rearrange("(p t) q -> p t q", t=PACK))
-        nc.sync.dma_start(idx3[:], offs3)
         nc.sync.dma_start(out=users_codes[:].bitcast(I32), in_=users_words[0].bitcast(I32))
         load_scale_rows([nc.sync] * 4, users_plane, users_scales)
         nc.sync.dma_start(out=keys_codes[:].bitcast(I32), in_=keys_words[0].bitcast(I32))
-        load_scale_rows([nc.sync] * 2 + [nc.gpsimd] * 2, keys_plane, keys_scales)
+        load_scale_rows([nc.sync] * 4, keys_plane, keys_scales)
+        nc.sync.dma_start(idx3[:], offs3)
         nc.sync.dma_start(idx[:], offs)
         nc.sync.dma_start(out=notes_codes[:].bitcast(I32), in_=notes_words[0].rearrange("p n t -> p (n t)").bitcast(I32))
         load_scale_rows([nc.sync] * 4, notes_plane, notes_scales)

from contextlib import ExitStack

import concourse.mybir as mybir
from concourse.masks import make_identity

D, K, T, Q, SLOTS = 512, 512, 1024, 128, 512
P = 128
PACK = 4
BANK = 512
HALF = SLOTS // 2
FLOPS = 2 * D * K * Q + 3 * 2 * K * Q * T

F32 = mybir.dt.float32
BF16 = mybir.dt.bfloat16
I32 = mybir.dt.int32
U32 = mybir.dt.uint32
U16 = mybir.dt.uint16
U8 = mybir.dt.uint8
FP8X4 = mybir.dt.float8_e4m3fn_x4
FP4X4 = mybir.dt.float4_e2m1fn_x4
ALU = mybir.AluOpType
COPY = mybir.ActivationFunctionType.Copy


def load_scale_rows(queues, plane, scales):
    for quadrant, queue in enumerate(queues):
        queue.dma_start(
            out=plane[32 * quadrant : 32 * quadrant + 4, :].bitcast(I32),
            in_=scales[0, 4 * quadrant : 4 * quadrant + 4, :].bitcast(I32),
        )


def tile_attend_twoerrands_madethree_kernel(
    tc, states, wq_words, wq_scales, keys_words, keys_scales, notes_words, notes_scales,
    users_words, users_scales, offs, offs2, offs3, offs4, offs5, offs6, out,
):
    nc = tc.nc
    with ExitStack() as ctx:
        sb = ctx.enter_context(tc.tile_pool(name="sb", bufs=1))
        reused = ctx.enter_context(tc.tile_pool(name="reused", bufs=1))
        ps = ctx.enter_context(tc.psum_pool(name="ps", bufs=1))

        states_raw = sb.tile([P, PACK, Q], F32, name="states_raw", align_bytes=64)
        wq_raw = sb.tile([P, K], U32, name="wq_raw", align_bytes=64)
        wq_plane_raw = sb.tile([P, K], U8, name="wq_plane_raw", align_bytes=64)
        keys_codes = sb.tile([P, 2 * T], U8, name="keys_codes", align_bytes=64)
        users_codes = sb.tile([P, 2 * T], U8, name="users_codes", align_bytes=64)
        notes_codes = sb.tile([P, T], U32, name="notes_codes", align_bytes=64)
        keys_plane = sb.tile([P, T], U8, name="keys_plane", align_bytes=64)
        users_plane = sb.tile([P, T], U8, name="users_plane", align_bytes=64)
        notes_plane = sb.tile([P, T], U8, name="notes_plane", align_bytes=64)
        lists = [sb.tile([P, SLOTS // 16], U16, name="list%d" % n) for n in range(6)]
        idx, idx2, idx3, idx4, idx5, idx6 = lists

        for plane in (wq_plane_raw, keys_plane):
            nc.gpsimd.memset(plane[:].bitcast(I32), 0)
        for plane in (users_plane, notes_plane):
            nc.vector.memset(plane[:].bitcast(I32), 0)
        f1 = sb.tile([P, T], F32, name="f1")
        f2 = sb.tile([P, T], F32, name="f2")
        nc.vector.memset(f2[:], 0.0)
        nc.vector.memset(f1[:], 0.0)

        nc.sync.dma_start(out=wq_raw[:].bitcast(I32), in_=wq_words[0].rearrange("p n t -> p (n t)").bitcast(I32))
        load_scale_rows([nc.sync] * 4, wq_plane_raw, wq_scales)
        nc.sync.dma_start(out=states_raw[:], in_=states.rearrange("(p t) q -> p t q", t=PACK))
        nc.sync.dma_start(out=users_codes[:].bitcast(I32), in_=users_words[0].bitcast(I32))
        load_scale_rows([nc.sync] * 4, users_plane, users_scales)
        nc.sync.dma_start(out=keys_codes[:].bitcast(I32), in_=keys_words[0].bitcast(I32))
        load_scale_rows([nc.sync] * 4, keys_plane, keys_scales)
        nc.sync.dma_start(idx3[:], offs3)
        nc.sync.dma_start(idx[:], offs)
        nc.sync.dma_start(out=notes_codes[:].bitcast(I32), in_=notes_words[0].rearrange("p n t -> p (n t)").bitcast(I32))
        load_scale_rows([nc.sync] * 4, notes_plane, notes_scales)
        nc.sync.dma_start(idx4[:], offs4)
        nc.sync.dma_start(idx2[:], offs2)
        nc.sync.dma_start(idx5[:], offs5)
        nc.sync.dma_start(idx6[:], offs6)

        wq_codes = sb.tile([P, K], U32, name="wq_codes", align_bytes=64)
        wq_plane = sb.tile([P, K], U8, name="wq_plane", align_bytes=64)
        nc.vector.tensor_copy(
            out=wq_plane[:].rearrange("p (t c i) -> p c t i", t=PACK, i=16),
            in_=wq_plane_raw[:].rearrange("p (c i t) -> p c t i", t=PACK, i=16),
        )
        nc.scalar.copy(
            out=wq_codes[:].rearrange("p (t c i) -> p c t i", t=PACK, i=4),
            in_=wq_raw[:].rearrange("p (c i t) -> p c t i", t=PACK, i=4),
        )

        states_bf = sb.tile([P, Q, PACK], BF16, name="states_bf", tag="states_bf", align_bytes=64)
        nc.vector.tensor_copy(
            out=states_bf[:].rearrange("p (c i) t -> p c t i", i=4),
            in_=states_raw[:].rearrange("p t (c i) -> p c t i", i=4),
        )
        states_codes = sb.tile([P, Q], U32, name="states_codes", align_bytes=64)
        states_plane = sb.tile([P, Q], U8, name="states_plane", align_bytes=64)
        nc.vector.quantize_mx(
            out=states_codes[:].bitcast(FP8X4), scales=states_plane[:],
            in_=states_bf[:].rearrange("p q t -> p (q t)"),
        )

        identity = sb.tile([P, P], F32, name="identity", tag="states_bf", align_bytes=64)
        make_identity(nc, identity[:])

        qv_ps = ps.tile([P, PACK, Q], F32, name="qv_ps", tag="bank0")
        for t in range(PACK):
            cols = slice(t * P, (t + 1) * P)
            nc.tensor.matmul_mx(
                out=qv_ps[:, t, :], lhsT=wq_codes[:, cols].bitcast(FP8X4), lhsT_scale=wq_plane[:, cols],
                rhs=states_codes[:].bitcast(FP8X4), rhs_scale=states_plane[:], start=True, stop=True,
            )
        qv_bf = sb.tile([P, Q, PACK], BF16, name="qv_bf", align_bytes=64)
        nc.scalar.copy(out=qv_bf[:], in_=qv_ps[:].rearrange("p t q -> p q t"))
        qv_codes = sb.tile([P, Q], U32, name="qv_codes", align_bytes=64)
        qv_plane = sb.tile([P, Q], U8, name="qv_plane", align_bytes=64)
        nc.vector.quantize_mx(
            out=qv_codes[:].bitcast(FP8X4), scales=qv_plane[:],
            in_=qv_bf[:].rearrange("p q t -> p (q t)"),
        )

        def scores(whole, pieces, codes, plane, table, table_plane, is_fp4):
            start = 0
            banks = []
            for width, engine, tag in pieces:
                bank = ps.tile([P, width], F32, name="scores_bank", tag=tag)
                if is_fp4:
                    moving = table[:, 2 * start : 2 * (start + width)].bitcast(FP4X4)
                else:
                    moving = table[:, start : start + width].bitcast(FP8X4)
                nc.tensor.matmul_mx(
                    out=bank[:], lhsT=codes[:].bitcast(FP8X4), lhsT_scale=plane[:],
                    rhs=moving, rhs_scale=table_plane[:, start : start + width], start=True, stop=True,
                )
                if engine == "vector":
                    nc.vector.tensor_copy(out=whole[:, start : start + width], in_=bank[:])
                else:
                    nc.scalar.copy(out=whole[:, start : start + width], in_=bank[:])
                start += width
                banks.append(bank)
            return banks

        lo, hi = slice(0, HALF), slice(HALF, SLOTS)
        lo16, hi16 = slice(0, HALF // 16), slice(HALF // 16, SLOTS // 16)

        c0 = sb.tile([P, T], F32, name="c0")
        c0_banks = scores(c0, [(BANK, "scalar", "bank1"), (BANK // 2, "vector", "bank2"), (BANK // 2, "scalar", "bank3")], states_codes, states_plane, users_codes, users_plane, True)
        c0_lo = sb.tile([P, HALF], F32, name="c0_lo")
        nc.scalar.activation(c0_lo[:], c0[:].indirect(idx3[:, lo16]), COPY)

        a = reused.tile([P, T], F32, name="a", align_bytes=64, offset=0)
        scores(a, [(BANK, "vector", "bank4"), (BANK // 2, "vector", "bank5"), (BANK // 2, "scalar", "bank6")], qv_codes, qv_plane, keys_codes, keys_plane, True)
        a_neg = sb.tile([P, SLOTS], F32, name="a_neg")
        nc.scalar.activation(a_neg[:, lo], a[:].indirect(idx[:, lo16]), COPY, scale=-1.0)
        nc.vector.tensor_scalar(a_neg[:, hi], a[:].indirect(idx[:, hi16]), -1.0, 0.0, ALU.mult, ALU.add)
        nc.vector.tensor_tensor(f2[:].indirect(idx4[:, lo16]), c0_lo[:], a_neg[:, lo], ALU.add)
        c0_hi = reused.tile([P, HALF], F32, name="c0_hi", align_bytes=64, offset=0)
        nc.scalar.activation(c0_hi[:], c0[:].indirect(idx3[:, hi16]), COPY)
        nc.vector.tensor_tensor(f2[:].indirect(idx4[:, hi16]), c0_hi[:], a_neg[:, hi], ALU.add)

        b = reused.tile([P, T], F32, name="b", align_bytes=64, offset=1024)
        scores(b, [(BANK, "scalar", "bank7"), (BANK // 2, "scalar", "bank0"), (BANK // 2, "vector", "bank3")], qv_codes, qv_plane, notes_codes, notes_plane, False)
        b_neg = sb.tile([P, SLOTS], F32, name="b_neg")
        nc.scalar.activation(b_neg[:], b[:].indirect(idx2[:]), COPY, scale=-1.0)
        a_picked = sb.tile([P, SLOTS], F32, name="a_picked")
        nc.scalar.activation(a_picked[:], a_neg[:], COPY, scale=-1.0)
        nc.vector.tensor_tensor(f1[:].indirect(idx3[:]), a_picked[:], b_neg[:], ALU.add)

        bb = sb.tile([P, T], F32, name="bb", tag="bb")
        bb_turned = sb.tile([P, T], F32, name="bb_turned")
        PIECE = 256
        turned = [ps.tile([P, PIECE], F32, name="turned%d" % n, tag=tag) for n, tag in enumerate(("bank3", "bank4", "bank5", "bank6"))]
        for term in (b, f2):
            for h in range(4):
                for j in range(2):
                    nc.tensor.matmul(
                        turned[h][:, j * P : (j + 1) * P], term[:, h * PIECE + j * P : h * PIECE + (j + 1) * P], identity[:],
                        start=(term is b and j == 0), stop=(term is f2 and j == 1), is_transpose=True,
                    )
        for h in range(4):
            nc.scalar.copy(out=bb_turned[:, h * PIECE : (h + 1) * PIECE], in_=turned[h][:])
        for h, tag in enumerate(("bank7", "bank0", "bank3", "bank4")):
            back = ps.tile([P, PIECE], F32, name="back%d" % h, tag=tag)
            for j in range(2):
                nc.tensor.transpose(back[:, j * P : (j + 1) * P], bb_turned[:, h * PIECE + j * P : h * PIECE + (j + 1) * P], identity[:])
            nc.scalar.copy(out=bb[:, h * PIECE : (h + 1) * PIECE], in_=back[:])
        cc = sb.tile([P, T], F32, name="cc")
        nc.vector.tensor_tensor(cc[:, 0:512], c0_banks[0][:], f1[:, 0:512], ALU.add)
        nc.vector.tensor_tensor(cc[:, 512:768], c0_banks[1][:], f1[:, 512:768], ALU.add)
        nc.gpsimd.tensor_tensor(cc[:, 768:1024], c0[:, 768:1024], f1[:, 768:1024], ALU.add)

        bb_picked = sb.tile([P, SLOTS], F32, name="bb_picked")
        nc.scalar.activation(bb_picked[:], bb[:].indirect(idx5[:]), COPY)
        cc_lo = sb.tile([P, HALF], F32, name="cc_lo")
        cc_hi = sb.tile([P, HALF], F32, name="cc_hi", tag="bb")
        nc.vector.tensor_copy(cc_lo[:], cc[:].indirect(idx6[:, lo16]))
        nc.scalar.activation(cc_hi[:], cc[:].indirect(idx6[:, hi16]), COPY)
        result = sb.tile([P, SLOTS], F32, name="result")
        for part, cc_picked in ((lo, cc_lo), (hi, cc_hi)):
            nc.vector.tensor_tensor(result[:, part], cc_picked[:], bb_picked[:, part], ALU.max)
            nc.sync.dma_start(out=out[:, part], in_=result[:, part])
